import numpy as np
import ml_dtypes


def mxq(x, axis, fmt="e4m3"):
    dtype, down = {"e4m3": (ml_dtypes.float8_e4m3fn, 7), "e5m2": (ml_dtypes.float8_e5m2, 14)}[fmt]
    v = np.moveaxis(np.asarray(x, np.float32).astype(ml_dtypes.bfloat16).astype(np.float64), axis, -1)
    blocks = v.reshape(v.shape[:-1] + (-1, 32))
    amax = np.abs(blocks).max(-1, keepdims=True)
    byte = np.maximum(np.where(amax > 0, np.frexp(amax)[1] - 1 + 127, 0) - down, 1)
    scale = np.exp2(byte - 127.0)
    codes = (blocks / scale).astype(np.float32).astype(dtype).astype(np.float64)
    return np.moveaxis((codes * scale).reshape(v.shape), -1, axis)


WIDE = False


def mx_kscale(k):
    if not WIDE:
        return np.ones(k)
    levels = np.array([10, -10, 5, -5, 0])
    if k % 512:
        return np.exp2(np.random.permutation(np.resize(levels, k // 32))).repeat(32)
    a = np.empty((k // 512, 16))
    for p in range(k // 512):
        a[p, :8] = np.random.permutation(np.resize(levels, 8))
        for g in range(8):
            far = levels[np.abs(levels - a[p, g]) >= 10]
            a[p, g + 8] = far[np.random.randint(len(far))]
    return np.exp2(a.ravel()).repeat(32)


def f64(x):
    return np.asarray(x).astype(np.float64)


def striped(idx):
    return np.tile(idx.reshape(-1, 16).T, (8, 1)).astype(np.uint16)


def unstriped(offs):
    return offs[:16].T.reshape(-1).astype(np.int64)


E2M1 = np.array([0.0, 0.5, 1.0, 1.5, 2.0, 3.0, 4.0, 6.0, -0.0, -0.5, -1.0, -1.5, -2.0, -3.0, -4.0, -6.0])


def pack_weight(w, fmt):
    k, n = w.shape
    w = f64(np.asarray(w, np.float32).astype(ml_dtypes.bfloat16)).reshape(k // 32, 32, n)
    amax = np.abs(w).max(1)
    if fmt == "e4m3":
        byte = np.frexp(amax)[1] - 1 + 127 - 7
    else:
        mant, ex = np.frexp(amax / 6.0)
        byte = np.where(mant > 0.5, ex, ex - 1) + 127
    byte = np.clip(np.where(amax > 0, byte, 1), 1, 254)
    scaled = (w * np.exp2(127.0 - byte)[:, None, :]).reshape(k, n).astype(np.float32)
    by_word = np.ascontiguousarray(scaled.reshape(k // 512, 128, 4, n).transpose(0, 1, 3, 2))
    if fmt == "e4m3":
        words = by_word.astype(ml_dtypes.float8_e4m3fn).view(np.uint8)
    else:
        c = by_word.astype(ml_dtypes.float4_e2m1fn).view(np.uint8) & 0xF
        words = (c[..., 0::2] | (c[..., 1::2] << 4)).reshape(k // 512, 128, 2 * n)
    return np.ascontiguousarray(words), np.ascontiguousarray(byte.astype(np.uint8).reshape(k // 512, 16, n))


def unpack_weight(words, scales, fmt):
    g, _, n = scales.shape
    words = np.ascontiguousarray(words).reshape(g, 128, n, -1)
    if fmt == "e4m3":
        vals = words.view(ml_dtypes.float8_e4m3fn).astype(np.float64)
    else:
        nib = np.empty((g, 128, n, 4), np.uint8)
        nib[..., 0::2] = words & 0xF
        nib[..., 1::2] = words >> 4
        vals = E2M1[nib]
    vals = vals * np.repeat(np.exp2(scales.astype(np.float64) - 127.0), 8, axis=1)[..., None]
    return vals.transpose(0, 1, 3, 2).reshape(g * 512, n)


def gelu(v):
    return 0.5 * v * (1.0 + np.tanh(np.sqrt(2.0 / np.pi) * (v + 0.044715 * v**3)))


def striped8(idx):
    return np.concatenate([v.reshape(-1, 16).T for v in idx]).astype(np.uint16)


def unstriped8(offs):
    return np.stack([offs[16 * g:16 * g + 16].T.reshape(-1) for g in range(8)]).astype(np.int64)


def put_heads(h, wgs, idx8, t2):
    r = np.arange(h.shape[0])
    page = np.zeros((h.shape[0], t2))
    page[r[:, None], idx8[r % 512 // 64]] = wgs[r // 4 % 128] * h
    return page


K, K2, T, S, H, T2, P, N = 1024, 512, 4096, 1024, 1024, 2048, 1024, 512


def setup_inputs():
    n = np.random.standard_normal
    s = mx_kscale(K)[:, None]
    u = mx_kscale(H)[:, None]
    tab_words, tab_scales = pack_weight(n((K, T)) * s, "e4m3")
    w2_words, w2_scales = pack_weight(1.6 * n((K2, H)) / np.sqrt(K) / s[K2:], "e2m1")
    w4_words, w4_scales = pack_weight(1.2 * n((H, N)) / np.sqrt(H) / u, "e4m3")
    return {
        "tab_words": tab_words, "tab_scales": tab_scales,
        "offs": striped(np.random.permutation(T)[:S]),
        "w1": (1.6 * n((K2, H)) / np.sqrt(K) / s[:K2]).astype(np.float32),
        "w2_words": w2_words, "w2_scales": w2_scales,
        "gain": (np.exp(0.3 * n(H)) * u[:, 0]).astype(np.float32),
        "wgs": np.repeat(np.random.uniform(0.5, 2.0, (8, S)), 16, axis=0).astype(np.float32),
        "offs2": striped8(np.stack([np.random.permutation(T2)[:S] for _ in range(8)])),
        "offs3": striped(np.random.permutation(T2)[:P]),
        "env": ((0.5 + n((H, P))) * u).astype(np.float32),
        "w3": (1.2 * n((H, N)) / np.sqrt(H) / u).astype(np.float32),
        "w4_words": w4_words, "w4_scales": w4_scales,
        "b3": (0.5 + 0.5 * n(N)).astype(np.float32),
    }


def reference(tab_words, tab_scales, offs, w1, w2_words, w2_scales, gain, wgs, offs2, offs3,
              env, w3, w4_words, w4_scales, b3):
    v = unpack_weight(tab_words, tab_scales, "e4m3")[:, unstriped(offs)]
    w1q = mxq(f64(w1), 0, "e4m3")
    w2q = unpack_weight(w2_words, w2_scales, "e2m1")
    a = w1q.T @ v[:K2] + w2q.T @ v[K2:]
    h = a / (1.0 + np.exp(-a)) * f64(gain)[:, None]
    page = put_heads(h, f64(wgs), unstriped8(offs2), T2)
    x = page[:, unstriped(offs3)]
    z = mxq(np.minimum(x, f64(env)), 0, "e4m3")
    y1 = mxq(f64(w3), 0, "e4m3").T @ z
    y2 = unpack_weight(w4_words, w4_scales, "e4m3").T @ z
    return np.maximum(y1 + f64(b3)[:, None], np.abs(y2))

@@ -1,0 +1,287 @@
+from contextlib import ExitStack
+
+import concourse.mybir as mybir
+
+F32 = mybir.dt.float32
+BF16 = mybir.dt.bfloat16
+I32 = mybir.dt.int32
+U32 = mybir.dt.uint32
+U16 = mybir.dt.uint16
+U8 = mybir.dt.uint8
+FP8X4 = mybir.dt.float8_e4m3fn_x4
+FP4X4 = mybir.dt.float4_e2m1fn_x4
+ALU = mybir.AluOpType
+ACT = mybir.ActivationFunctionType
+
+P = 128
+PACK = 4
+K_PASS = 512
+T, S, H, T2, M, N = 4096, 1024, 1024, 2048, 1024, 512
+HALF = 512
+CHUNK = 256
+SLICES = H // P
+BANKS = 8
+
+FLOPS = 2 * 1024 * H * S + 2 * 2 * H * N * M
+
+
+def tile_list_mode_pick_scores_kernel(
+    tc, tab_words, tab_scales, offs, w1, w2_words, w2_scales, gain, wgs, offs2, offs3,
+    env, w3, w4_words, w4_scales, b3, out,
+):
+    nc = tc.nc
+    with ExitStack() as ctx:
+        lists = ctx.enter_context(tc.tile_pool(name="lists", bufs=1))
+        keep = ctx.enter_context(tc.tile_pool(name="keep", bufs=1))
+        ring = ctx.enter_context(tc.tile_pool(name="ring", bufs=2))
+        psum = ctx.enter_context(tc.psum_pool(name="psum", bufs=1))
+
+        def load_list(src, name):
+            tile = lists.tile([P, S // 16], U16, name=name)
+            nc.sync.dma_start(tile[:], src)
+            return tile
+
+        def load_scale_rows(queue, tile, src, passes):
+            for q in range(4):
+                queue.dma_start(
+                    tile[32 * q : 32 * q + 4, :].bitcast(I32).rearrange("r (a c) -> r a c", a=passes),
+                    src[:, 4 * q : 4 * q + 4, :].rearrange("a r c -> r a c").bitcast(I32),
+                )
+
+        def bank(i):
+            return psum.tile([P, HALF], F32, tag="bank%d" % (i % BANKS), name="bank%d" % (i % BANKS))
+
+        idx1 = load_list(offs, "idx1")
+        idx2 = load_list(offs2, "idx2")
+        idx3 = load_list(offs3, "idx3")
+
+        tab_sc = keep.tile([P, 2 * T], U8, tag="tab_sc", name="tab_sc", align_bytes=64)
+        nc.vector.memset(tab_sc[:].bitcast(I32), 0)
+        load_scale_rows(nc.scalar, tab_sc, tab_scales, 2)
+
+        w2_sc_raw = keep.tile([P, H], U8, tag="small_sc", name="w2_sc_raw", align_bytes=64)
+        nc.vector.memset(w2_sc_raw[:].bitcast(I32), 0)
+        load_scale_rows(nc.gpsimd, w2_sc_raw, w2_scales, 1)
+
+        gain_t = keep.tile([P, 2, PACK], F32, name="gain_t")
+        nc.sync.dma_start(gain_t[:], gain.rearrange("(b p i) -> p b i", b=2, i=PACK))
+
+        w2_raw = keep.tile([P, 2 * H], U8, tag="w2_raw", name="w2_raw")
+        nc.sync.dma_start(w2_raw[:].bitcast(I32), w2_words[0].bitcast(I32))
+
+        def load_tab(a):
+            tile = keep.tile([P, T], I32, tag="big%d" % a, name="tab%d" % a)
+            nc.sync.dma_start(tile[:], tab_words[a].rearrange("p t i -> p (t i)").bitcast(I32))
+            return tile
+
+        def load_weight(src, name):
+            raw = keep.tile([P, PACK, HALF], F32, tag="w_raw", name=name)
+            nc.sync.dma_start(raw[:], src.rearrange("(p j) c -> p j c", j=PACK))
+            return raw
+
+        def quantize(src, words, name):
+            codes = keep.tile([P, words], U32, name=name + "_codes", align_bytes=64)
+            scales = keep.tile([P, words], U8, name=name + "_scales", align_bytes=64)
+            nc.vector.quantize_mx(out=codes[:].bitcast(FP8X4), scales=scales[:], in_=src[:])
+            return codes, scales
+
+        def round_w1(raw, name):
+            grouped = ring.tile([P, HALF * PACK], BF16, tag="w_bf", name=name, align_bytes=64)
+            nc.scalar.copy(
+                grouped[:].rearrange("p (t m j) -> p m j t", t=PACK, j=PACK),
+                raw[:].rearrange("p j (m t) -> p m j t", t=PACK),
+            )
+            return grouped
+
+        def round_w3(raw, name):
+            grouped = ring.tile([P, HALF * PACK], BF16, tag="w_bf", name=name, align_bytes=64)
+            nc.scalar.copy(
+                grouped[:].rearrange("p (c i j) -> p c j i", i=PACK, j=PACK),
+                raw[:].rearrange("p j (c i) -> p c j i", i=PACK),
+            )
+            return grouped
+
+        tab = [load_tab(0)]
+        w1_raw = load_weight(w1[:, 0:HALF], "w1_raw0")
+        tab.append(load_tab(1))
+        wgs_t = keep.tile([P, S], F32, name="wgs_t")
+        nc.sync.dma_start(wgs_t[:], wgs)
+
+        pages = []
+        for i in range(2):
+            page = keep.tile([P, T2], F32, name="page%d" % i)
+            nc.vector.memset(page[:], 0.0)
+            pages.append(page)
+
+        w2_codes = keep.tile([P, 2 * H], U8, name="w2_codes", align_bytes=64)
+        nc.vector.tensor_copy(
+            w2_codes[:].rearrange("p (b t m e) -> p b t m e", b=2, t=PACK, e=2),
+            w2_raw[:].rearrange("p (b m t e) -> p b t m e", b=2, t=PACK, e=2),
+        )
+        w2_sc = keep.tile([P, H], U8, name="w2_sc", align_bytes=64)
+        nc.vector.tensor_copy(
+            w2_sc[:].rearrange("p (b t m) -> p b t m", b=2, t=PACK),
+            w2_sc_raw[:].rearrange("p (b m t) -> p b t m", b=2, t=PACK),
+        )
+
+        v_codes, v_scales = {}, {}
+
+        def gather_words(a, h):
+            cols = idx1[:, h * (HALF // 16) : (h + 1) * (HALF // 16)]
+            tile = keep.tile([P, HALF], U32, name="v_codes%d%d" % (a, h), align_bytes=64)
+            nc.vector.tensor_copy(tile[:], tab[a][:].bitcast(U32).indirect(cols))
+            v_codes[a, h] = tile
+
+        def gather_scales(a, h):
+            cols = idx1[:, h * (HALF // 16) : (h + 1) * (HALF // 16)]
+            tile = keep.tile([P, HALF], U8, name="v_scales%d%d" % (a, h), align_bytes=64)
+            nc.vector.tensor_copy(tile[:], tab_sc[:, a * T : (a + 1) * T].indirect(cols))
+            v_scales[a, h] = tile
+
+        w1_q = [quantize(round_w1(w1_raw, "w1_bf0"), HALF, "w1_0")]
+        for h in range(2):
+            gather_words(0, h)
+            gather_scales(0, h)
+            gather_scales(1, h)
+            gather_words(1, h)
+
+        w1_raw = load_weight(w1[:, HALF:H], "w1_raw1")
+
+        def load_env(b):
+            tile = keep.tile([P, PACK, M], F32, tag="big%d" % b, name="env%d" % b)
+            nc.sync.dma_start(tile[:], env[b * K_PASS : (b + 1) * K_PASS, :].rearrange("(p i) m -> p i m", i=PACK))
+            return tile
+
+        def features(s):
+            b, t = divmod(s, PACK)
+            codes, scales = w1_q[b]
+            cols = slice(t * P, (t + 1) * P)
+            weight = ring.tile([P, S], F32, tag="weight", name="weight")
+            nc.scalar.activation(weight[:], wgs_t[:], ACT.Copy, scale=gain_t[:, b, t : t + 1])
+            act = ring.tile([P, S], F32, tag="act", name="act", bufs=3)
+            for h in range(2):
+                acc = bank(2 * s + h)
+                nc.tensor.matmul_mx(
+                    out=acc[:], lhsT=codes[:, cols].bitcast(FP8X4), lhsT_scale=scales[:, cols],
+                    rhs=v_codes[0, h][:].bitcast(FP8X4), rhs_scale=v_scales[0, h][:],
+                    start=True, stop=False,
+                )
+                nc.tensor.matmul_mx(
+                    out=acc[:], lhsT=w2_codes[:, 2 * s * P : 2 * (s + 1) * P].bitcast(FP4X4),
+                    lhsT_scale=w2_sc[:, s * P : (s + 1) * P],
+                    rhs=v_codes[1, h][:].bitcast(FP8X4), rhs_scale=v_scales[1, h][:],
+                    start=False, stop=True,
+                )
+                nc.scalar.activation(act[:, h * HALF : (h + 1) * HALF], acc[:], ACT.Silu)
+            return act, weight
+
+        def scatter(s, pieces):
+            act, weight = features(s)
+            width = S // pieces
+            for c in range(pieces):
+                cols = slice(c * width, (c + 1) * width)
+                places = idx2[:, c * (width // 16) : (c + 1) * (width // 16)]
+                nc.vector.tensor_tensor(pages[s % 2][:].indirect(places), act[:, cols], weight[:, cols], ALU.mult)
+
+        picked = [keep.tile([P, PACK, M], F32, name="picked%d" % b) for b in range(2)]
+
+        def pick(s, lo, hi):
+            b, t = divmod(s, PACK)
+            nc.vector.tensor_copy(picked[b][:, t, lo:hi], pages[s % 2][:].indirect(idx3[:, lo // 16 : hi // 16]))
+
+        def limit(b, lo, hi, name):
+            z = keep.tile([P, (hi - lo) * PACK], BF16, name=name, align_bytes=64)
+            nc.vector.tensor_tensor(
+                z[:].rearrange("p (c i t) -> p c t i", i=PACK, t=PACK),
+                picked[b][:, :, lo:hi].rearrange("p t (c i) -> p c t i", i=PACK),
+                env_t[b][:, :, lo:hi].rearrange("p t (c i) -> p c t i", i=PACK),
+                ALU.min,
+            )
+            return z
+
+        scatter(0, 2)
+        scatter(1, 1)
+        w1_q.append(quantize(round_w1(w1_raw, "w1_bf1"), HALF, "w1_1"))
+        env_t = [load_env(0)]
+        w3_raw = load_weight(w3[0:K_PASS, :], "w3_raw0")
+        w4_t = keep.tile([P, 2, N], I32, tag="tab_sc", name="w4_t", align_bytes=64)
+        nc.sync.dma_start(w4_t[:], w4_words.rearrange("a p c i -> p a (c i)").bitcast(I32))
+        w4_sc = keep.tile([P, 2 * N], U8, tag="small_sc", name="w4_sc", align_bytes=64)
+        nc.vector.memset(w4_sc[:].bitcast(I32), 0)
+        load_scale_rows(nc.sync, w4_sc, w4_scales, 2)
+        b3_t = keep.tile([P, N // P], F32, tag="w2_raw", name="b3_t")
+        with nc.allow_non_contiguous_dma(reason="one bias value a partition"):
+            nc.sync.dma_start(b3_t[:], b3.rearrange("(j p) -> p j", p=P))
+        pick(0, 0, M)
+        pick(1, 0, M)
+        scatter(2, 1)
+        scatter(3, 1)
+        w3_q = [quantize(round_w3(w3_raw, "w3_bf0"), N, "w3_0")]
+        w3_raw = load_weight(w3[K_PASS:H, :], "w3_raw1")
+        env_t.append(load_env(1))
+        pick(2, 0, M)
+        pick(3, 0, M)
+        scatter(4, 1)
+        z0 = limit(0, 0, M, "z0")
+        scatter(5, 1)
+        z0_q = quantize(z0, M, "z0")
+        w3_q.append(quantize(round_w3(w3_raw, "w3_bf1"), N, "w3_1"))
+        pick(4, 0, M)
+        pick(5, 0, M)
+        scatter(6, 1)
+        scatter(7, 1)
+        pick(6, 0, M)
+
+        def score_pass(acc, b, j, z_codes, z_scales):
+            cols = slice(j * P, (j + 1) * P)
+            nc.tensor.matmul_mx(
+                out=acc[:, 0:CHUNK], lhsT=w3_q[b][0][:, cols].bitcast(FP8X4), lhsT_scale=w3_q[b][1][:, cols],
+                rhs=z_codes.bitcast(FP8X4), rhs_scale=z_scales, start=(b == 0), stop=False,
+            )
+            nc.tensor.matmul_mx(
+                out=acc[:, CHUNK : 2 * CHUNK], lhsT=w4_t[:, b, cols].bitcast(FP8X4),
+                lhsT_scale=w4_sc[:, b * N + j * P : b * N + (j + 1) * P],
+                rhs=z_codes.bitcast(FP8X4), rhs_scale=z_scales, start=False, stop=(b == 1),
+            )
+
+        tiles_n = N // P
+        chunks = M // CHUNK
+        accs = {}
+
+        def open_scores(c):
+            for j in range(tiles_n):
+                accs[c, j] = bank(c * tiles_n + j)
+                lo = c * CHUNK
+                score_pass(accs[c, j], 0, j, z0_q[0][:, lo : lo + CHUNK], z0_q[1][:, lo : lo + CHUNK])
+
+        def close_scores(c, z_q):
+            for j in range(tiles_n):
+                score_pass(accs[c, j], 1, j, z_q[0][:], z_q[1][:])
+
+        def finish(c):
+            for j in range(tiles_n):
+                size = ring.tile([P, CHUNK], F32, tag="size", name="size", bufs=4)
+                nc.scalar.activation(size[:], accs[c, j][:, CHUNK : 2 * CHUNK], ACT.Abs)
+                res = ring.tile([P, CHUNK], F32, tag="res", name="res", bufs=8)
+                nc.vector.scalar_tensor_tensor(
+                    res[:], accs[c, j][:, 0:CHUNK], b3_t[:, j : j + 1], size[:], ALU.add, ALU.max
+                )
+                nc.sync.dma_start(out[j * P : (j + 1) * P, c * CHUNK : (c + 1) * CHUNK], res[:])
+
+        open_scores(0)
+        open_scores(1)
+        z1 = {}
+        pick(7, 0, CHUNK)
+        for c in range(chunks + 1):
+            if c + 1 < chunks:
+                pick(7, (c + 1) * CHUNK, (c + 2) * CHUNK)
+            if c < chunks:
+                z1[c] = limit(1, c * CHUNK, (c + 1) * CHUNK, "z1_%d" % c)
+            if c >= 1:
+                z_q = quantize(z1[c - 1], CHUNK, "z1_%d" % (c - 1))
+                if c - 1 >= 2:
+                    finish(c - 3)
+                    open_scores(c - 1)
+                close_scores(c - 1, z_q)
+        finish(chunks - 2)
+        finish(chunks - 1)

@@ -54,19 +54,18 @@ def tile_list_mode_pick_scores_kernel(
         idx1 = load_list(offs, "idx1")
         idx2 = load_list(offs2, "idx2")
         idx3 = load_list(offs3, "idx3")
-
-        tab_sc = keep.tile([P, 2 * T], U8, tag="tab_sc", name="tab_sc", align_bytes=64)
-        nc.vector.memset(tab_sc[:].bitcast(I32), 0)
-        load_scale_rows(nc.scalar, tab_sc, tab_scales, 2)
-
-        w2_sc_raw = keep.tile([P, H], U8, tag="small_sc", name="w2_sc_raw", align_bytes=64)
-        nc.vector.memset(w2_sc_raw[:].bitcast(I32), 0)
-        load_scale_rows(nc.gpsimd, w2_sc_raw, w2_scales, 1)
-
         gain_t = keep.tile([P, 2, PACK], F32, name="gain_t")
         nc.sync.dma_start(gain_t[:], gain.rearrange("(b p i) -> p b i", b=2, i=PACK))
 
-        w2_raw = keep.tile([P, 2 * H], U8, tag="w2_raw", name="w2_raw")
+        tab_sc = keep.tile([P, 2 * T], U8, tag="stage", name="tab_sc", align_bytes=64)
+        nc.vector.memset(tab_sc[:].bitcast(I32), 0)
+        load_scale_rows(nc.scalar, tab_sc, tab_scales, 2)
+
+        w2_sc_raw = keep.tile([P, H], U8, tag="small", name="w2_sc_raw", align_bytes=64)
+        nc.vector.memset(w2_sc_raw[:].bitcast(I32), 0)
+        load_scale_rows(nc.scalar, w2_sc_raw, w2_scales, 1)
+
+        w2_raw = keep.tile([P, 2 * H], U8, tag="big1", name="w2_raw")
         nc.sync.dma_start(w2_raw[:].bitcast(I32), w2_words[0].bitcast(I32))
 
         def load_tab(a):
@@ -74,14 +73,14 @@ def tile_list_mode_pick_scores_kernel(
             nc.sync.dma_start(tile[:], tab_words[a].rearrange("p t i -> p (t i)").bitcast(I32))
             return tile
 
-        def load_weight(src, name):
-            raw = keep.tile([P, PACK, HALF], F32, tag="w_raw", name=name)
+        def load_weight(src, name, tag):
+            raw = keep.tile([P, PACK, HALF], F32, tag=tag, name=name, align_bytes=64)
             nc.sync.dma_start(raw[:], src.rearrange("(p j) c -> p j c", j=PACK))
             return raw
 
         def quantize(src, words, name):
-            codes = keep.tile([P, words], U32, name=name + "_codes", align_bytes=64)
-            scales = keep.tile([P, words], U8, name=name + "_scales", align_bytes=64)
+            codes = keep.tile([P, words], U32, tag=name + "_codes", name=name + "_codes", align_bytes=64)
+            scales = keep.tile([P, words], U8, tag=name + "_scales", name=name + "_scales", align_bytes=64)
             nc.vector.quantize_mx(out=codes[:].bitcast(FP8X4), scales=scales[:], in_=src[:])
             return codes, scales
 
@@ -102,10 +101,7 @@ def tile_list_mode_pick_scores_kernel(
             return grouped
 
         tab = [load_tab(0)]
-        w1_raw = load_weight(w1[:, 0:HALF], "w1_raw0")
-        tab.append(load_tab(1))
-        wgs_t = keep.tile([P, S], F32, name="wgs_t")
-        nc.sync.dma_start(wgs_t[:], wgs)
+        w1_raw = load_weight(w1[:, 0:HALF], "w1_raw0", "first")
 
         pages = []
         for i in range(2):
@@ -118,6 +114,7 @@ def tile_list_mode_pick_scores_kernel(
             w2_codes[:].rearrange("p (b t m e) -> p b t m e", b=2, t=PACK, e=2),
             w2_raw[:].rearrange("p (b m t e) -> p b t m e", b=2, t=PACK, e=2),
         )
+        tab.append(load_tab(1))
         w2_sc = keep.tile([P, H], U8, name="w2_sc", align_bytes=64)
         nc.vector.tensor_copy(
             w2_sc[:].rearrange("p (b t m) -> p b t m", b=2, t=PACK),
@@ -139,26 +136,30 @@ def tile_list_mode_pick_scores_kernel(
             v_scales[a, h] = tile
 
         w1_q = [quantize(round_w1(w1_raw, "w1_bf0"), HALF, "w1_0")]
+        wgs_t = keep.tile([P, S], F32, tag="first", name="wgs_t", align_bytes=64)
+        nc.sync.dma_start(wgs_t[:], wgs)
         for h in range(2):
-            gather_words(0, h)
             gather_scales(0, h)
             gather_scales(1, h)
+            gather_words(0, h)
             gather_words(1, h)
 
-        w1_raw = load_weight(w1[:, HALF:H], "w1_raw1")
+        w1_raw = load_weight(w1[:, HALF:H], "w1_raw1", "stage")
 
         def load_env(b):
             tile = keep.tile([P, PACK, M], F32, tag="big%d" % b, name="env%d" % b)
             nc.sync.dma_start(tile[:], env[b * K_PASS : (b + 1) * K_PASS, :].rearrange("(p i) m -> p i m", i=PACK))
             return tile
 
-        def features(s):
+        picked = [keep.tile([P, PACK, M], F32, name="picked%d" % b) for b in range(2)]
+
+        def features(s, pieces):
             b, t = divmod(s, PACK)
             codes, scales = w1_q[b]
             cols = slice(t * P, (t + 1) * P)
-            weight = ring.tile([P, S], F32, tag="weight", name="weight")
-            nc.scalar.activation(weight[:], wgs_t[:], ACT.Copy, scale=gain_t[:, b, t : t + 1])
-            act = ring.tile([P, S], F32, tag="act", name="act", bufs=3)
+            act = picked[b][:, t ^ 1, :]
+            feat = ring.tile([P, S], F32, tag="feat", name="feat", bufs=3)
+            width = S // pieces
             for h in range(2):
                 acc = bank(2 * s + h)
                 nc.tensor.matmul_mx(
@@ -173,17 +174,18 @@ def tile_list_mode_pick_scores_kernel(
                     start=False, stop=True,
                 )
                 nc.scalar.activation(act[:, h * HALF : (h + 1) * HALF], acc[:], ACT.Silu)
-            return act, weight
+                if ((h + 1) * HALF) % width == 0:
+                    done = slice((h + 1) * HALF - width, (h + 1) * HALF)
+                    nc.scalar.activation(feat[:, done], act[:, done], ACT.Copy, scale=gain_t[:, b, t : t + 1])
+            return feat
 
         def scatter(s, pieces):
-            act, weight = features(s)
+            feat = features(s, pieces)
             width = S // pieces
             for c in range(pieces):
                 cols = slice(c * width, (c + 1) * width)
                 places = idx2[:, c * (width // 16) : (c + 1) * (width // 16)]
-                nc.vector.tensor_tensor(pages[s % 2][:].indirect(places), act[:, cols], weight[:, cols], ALU.mult)
-
-        picked = [keep.tile([P, PACK, M], F32, name="picked%d" % b) for b in range(2)]
+                nc.vector.tensor_tensor(pages[s % 2][:].indirect(places), feat[:, cols], wgs_t[:, cols], ALU.mult)
 
         def pick(s, lo, hi):
             b, t = divmod(s, PACK)
@@ -203,21 +205,21 @@ def tile_list_mode_pick_scores_kernel(
         scatter(1, 1)
         w1_q.append(quantize(round_w1(w1_raw, "w1_bf1"), HALF, "w1_1"))
         env_t = [load_env(0)]
-        w3_raw = load_weight(w3[0:K_PASS, :], "w3_raw0")
-        w4_t = keep.tile([P, 2, N], I32, tag="tab_sc", name="w4_t", align_bytes=64)
-        nc.sync.dma_start(w4_t[:], w4_words.rearrange("a p c i -> p a (c i)").bitcast(I32))
-        w4_sc = keep.tile([P, 2 * N], U8, tag="small_sc", name="w4_sc", align_bytes=64)
-        nc.vector.memset(w4_sc[:].bitcast(I32), 0)
-        load_scale_rows(nc.sync, w4_sc, w4_scales, 2)
-        b3_t = keep.tile([P, N // P], F32, tag="w2_raw", name="b3_t")
-        with nc.allow_non_contiguous_dma(reason="one bias value a partition"):
-            nc.sync.dma_start(b3_t[:], b3.rearrange("(j p) -> p j", p=P))
+        w3_raw = load_weight(w3[0:K_PASS, :], "w3_raw0", "stage")
         pick(0, 0, M)
         pick(1, 0, M)
         scatter(2, 1)
         scatter(3, 1)
+        w4_t = keep.tile([P, 2, N], I32, tag="w1_0_codes", name="w4_t", align_bytes=64)
+        nc.sync.dma_start(w4_t[:], w4_words.rearrange("a p c i -> p a (c i)").bitcast(I32))
+        w4_sc = keep.tile([P, 2 * N], U8, tag="w1_0_scales", name="w4_sc", align_bytes=64)
+        nc.vector.memset(w4_sc[:].bitcast(I32), 0)
+        load_scale_rows(nc.sync, w4_sc, w4_scales, 2)
+        b3_t = keep.tile([P, N // P], F32, tag="small", name="b3_t", align_bytes=64)
+        with nc.allow_non_contiguous_dma(reason="one bias value a partition"):
+            nc.sync.dma_start(b3_t[:], b3.rearrange("(j p) -> p j", p=P))
         w3_q = [quantize(round_w3(w3_raw, "w3_bf0"), N, "w3_0")]
-        w3_raw = load_weight(w3[K_PASS:H, :], "w3_raw1")
+        w3_raw = load_weight(w3[K_PASS:H, :], "w3_raw1", "stage")
         env_t.append(load_env(1))
         pick(2, 0, M)
         pick(3, 0, M)

@@ -42,10 +42,10 @@ def tile_list_mode_pick_scores_kernel(
             return tile
 
         def load_scale_rows(queue, tile, src, passes):
-            for q in range(4):
+            for r in range(4):
                 queue.dma_start(
-                    tile[32 * q : 32 * q + 4, :].bitcast(I32).rearrange("r (a c) -> r a c", a=passes),
-                    src[:, 4 * q : 4 * q + 4, :].rearrange("a r c -> r a c").bitcast(I32),
+                    tile[r:P:32, :].bitcast(I32).rearrange("q (a c) -> q a c", a=passes),
+                    src[:, r:16:4, :].rearrange("a q c -> q a c").bitcast(I32),
                 )
 
         def bank(i):
@@ -57,9 +57,10 @@ def tile_list_mode_pick_scores_kernel(
         gain_t = keep.tile([P, 2, PACK], F32, name="gain_t")
         nc.sync.dma_start(gain_t[:], gain.rearrange("(b p i) -> p b i", b=2, i=PACK))
 
-        tab_sc = keep.tile([P, 2 * T], U8, tag="stage", name="tab_sc", align_bytes=64)
+        tab_sc = keep.tile([P, T], U8, tag="stage", name="tab_sc", align_bytes=64)
         nc.vector.memset(tab_sc[:].bitcast(I32), 0)
-        load_scale_rows(nc.scalar, tab_sc, tab_scales, 2)
+        nc.scalar.dma_start(tab_sc[4:P:8, :].bitcast(I32), tab_scales[0].bitcast(I32))
+        load_scale_rows(nc.scalar, tab_sc, tab_scales[1:2], 1)
 
         w2_sc_raw = keep.tile([P, H], U8, tag="small", name="w2_sc_raw", align_bytes=64)
         nc.vector.memset(w2_sc_raw[:].bitcast(I32), 0)
@@ -121,7 +122,7 @@ def tile_list_mode_pick_scores_kernel(
             w2_sc_raw[:].rearrange("p (b m t) -> p b t m", b=2, t=PACK),
         )
 
-        v_codes, v_scales = {}, {}
+        v_codes = {}
 
         def gather_words(a, h):
             cols = idx1[:, h * (HALF // 16) : (h + 1) * (HALF // 16)]
@@ -129,18 +130,17 @@ def tile_list_mode_pick_scores_kernel(
             nc.vector.tensor_copy(tile[:], tab[a][:].bitcast(U32).indirect(cols))
             v_codes[a, h] = tile
 
-        def gather_scales(a, h):
-            cols = idx1[:, h * (HALF // 16) : (h + 1) * (HALF // 16)]
-            tile = keep.tile([P, HALF], U8, name="v_scales%d%d" % (a, h), align_bytes=64)
-            nc.vector.tensor_copy(tile[:], tab_sc[:, a * T : (a + 1) * T].indirect(cols))
-            v_scales[a, h] = tile
+        picked_sc = keep.tile([P, S], U8, name="picked_sc", align_bytes=64)
+        nc.vector.tensor_copy(picked_sc[:], tab_sc[:].indirect(idx1[:]))
+        v_sc = keep.tile([P, S], U8, name="v_sc", align_bytes=64)
+        nc.vector.memset(v_sc[:].bitcast(I32), 0)
+        for r in range(4):
+            nc.scalar.dma_start(v_sc[r:P:32, :].bitcast(I32), picked_sc[4 + 8 * r : P : 32, :].bitcast(I32))
 
         w1_q = [quantize(round_w1(w1_raw, "w1_bf0"), HALF, "w1_0")]
         wgs_t = keep.tile([P, S], F32, tag="first", name="wgs_t", align_bytes=64)
         nc.sync.dma_start(wgs_t[:], wgs)
         for h in range(2):
-            gather_scales(0, h)
-            gather_scales(1, h)
             gather_words(0, h)
             gather_words(1, h)
 
@@ -153,39 +153,39 @@ def tile_list_mode_pick_scores_kernel(
 
         picked = [keep.tile([P, PACK, M], F32, name="picked%d" % b) for b in range(2)]
 
-        def features(s, pieces):
+        used_banks = []
+
+        def features(s, lo, hi, feat):
             b, t = divmod(s, PACK)
             codes, scales = w1_q[b]
             cols = slice(t * P, (t + 1) * P)
             act = picked[b][:, t ^ 1, :]
-            feat = ring.tile([P, S], F32, tag="feat", name="feat", bufs=3)
-            width = S // pieces
-            for h in range(2):
-                acc = bank(2 * s + h)
+            for first in range(lo, hi, HALF):
+                last = min(first + HALF, hi)
+                h, start = divmod(first, HALF)
+                part = slice(start, start + last - first)
+                acc = bank(len(used_banks))
+                used_banks.append(acc)
                 nc.tensor.matmul_mx(
-                    out=acc[:], lhsT=codes[:, cols].bitcast(FP8X4), lhsT_scale=scales[:, cols],
-                    rhs=v_codes[0, h][:].bitcast(FP8X4), rhs_scale=v_scales[0, h][:],
+                    out=acc[:, 0 : last - first], lhsT=codes[:, cols].bitcast(FP8X4), lhsT_scale=scales[:, cols],
+                    rhs=v_codes[0, h][:, part].bitcast(FP8X4), rhs_scale=v_sc[:, first:last],
                     start=True, stop=False,
                 )
                 nc.tensor.matmul_mx(
-                    out=acc[:], lhsT=w2_codes[:, 2 * s * P : 2 * (s + 1) * P].bitcast(FP4X4),
+                    out=acc[:, 0 : last - first], lhsT=w2_codes[:, 2 * s * P : 2 * (s + 1) * P].bitcast(FP4X4),
                     lhsT_scale=w2_sc[:, s * P : (s + 1) * P],
-                    rhs=v_codes[1, h][:].bitcast(FP8X4), rhs_scale=v_scales[1, h][:],
+                    rhs=v_codes[1, h][:, part].bitcast(FP8X4), rhs_scale=picked_sc[:, first:last],
                     start=False, stop=True,
                 )
-                nc.scalar.activation(act[:, h * HALF : (h + 1) * HALF], acc[:], ACT.Silu)
-                if ((h + 1) * HALF) % width == 0:
-                    done = slice((h + 1) * HALF - width, (h + 1) * HALF)
-                    nc.scalar.activation(feat[:, done], act[:, done], ACT.Copy, scale=gain_t[:, b, t : t + 1])
-            return feat
+                nc.scalar.activation(act[:, first:last], acc[:, 0 : last - first], ACT.Silu)
+            nc.scalar.activation(feat[:, lo:hi], act[:, lo:hi], ACT.Copy, scale=gain_t[:, b, t : t + 1])
 
-        def scatter(s, pieces):
-            feat = features(s, pieces)
-            width = S // pieces
-            for c in range(pieces):
-                cols = slice(c * width, (c + 1) * width)
-                places = idx2[:, c * (width // 16) : (c + 1) * (width // 16)]
-                nc.vector.tensor_tensor(pages[s % 2][:].indirect(places), feat[:, cols], wgs_t[:, cols], ALU.mult)
+        def scatter(s, cuts):
+            feat = ring.tile([P, S], F32, tag="feat", name="feat", bufs=3)
+            for lo, hi in zip(cuts, cuts[1:]):
+                features(s, lo, hi, feat)
+                places = idx2[:, lo // 16 : hi // 16]
+                nc.vector.tensor_tensor(pages[s % 2][:].indirect(places), feat[:, lo:hi], wgs_t[:, lo:hi], ALU.mult)
 
         def pick(s, lo, hi):
             b, t = divmod(s, PACK)
@@ -201,15 +201,15 @@ def tile_list_mode_pick_scores_kernel(
             )
             return z
 
-        scatter(0, 2)
-        scatter(1, 1)
+        scatter(0, (0, CHUNK, HALF, S))
+        scatter(1, (0, S))
         w1_q.append(quantize(round_w1(w1_raw, "w1_bf1"), HALF, "w1_1"))
         env_t = [load_env(0)]
         w3_raw = load_weight(w3[0:K_PASS, :], "w3_raw0", "stage")
         pick(0, 0, M)
         pick(1, 0, M)
-        scatter(2, 1)
-        scatter(3, 1)
+        scatter(2, (0, S))
+        scatter(3, (0, S))
         w4_t = keep.tile([P, 2, N], I32, tag="w1_0_codes", name="w4_t", align_bytes=64)
         nc.sync.dma_start(w4_t[:], w4_words.rearrange("a p c i -> p a (c i)").bitcast(I32))
         w4_sc = keep.tile([P, 2 * N], U8, tag="w1_0_scales", name="w4_sc", align_bytes=64)
@@ -223,15 +223,15 @@ def tile_list_mode_pick_scores_kernel(
         env_t.append(load_env(1))
         pick(2, 0, M)
         pick(3, 0, M)
-        scatter(4, 1)
+        scatter(4, (0, S))
         z0 = limit(0, 0, M, "z0")
-        scatter(5, 1)
+        scatter(5, (0, S))
         z0_q = quantize(z0, M, "z0")
         w3_q.append(quantize(round_w3(w3_raw, "w3_bf1"), N, "w3_1"))
         pick(4, 0, M)
         pick(5, 0, M)
-        scatter(6, 1)
-        scatter(7, 1)
+        scatter(6, (0, S))
+        scatter(7, (0, S))
         pick(6, 0, M)
 
         def score_pass(acc, b, j, z_codes, z_scales):

@@ -15,14 +15,15 @@ ACT = mybir.ActivationFunctionType
 
 P = 128
 PACK = 4
-K_PASS = 512
-T, S, H, T2, M, N = 4096, 1024, 1024, 2048, 1024, 512
-HALF = 512
-CHUNK = 256
-SLICES = H // P
+K_PASS = P * PACK
+GROUP = 16
+K, T, S, H, T2, M, N = 1024, 4096, 1024, 1024, 2048, 1024, 512
+BANK = 512
 BANKS = 8
+CHUNK = BANK // 2
+SLICES = H // P
 
-FLOPS = 2 * 1024 * H * S + 2 * 2 * H * N * M
+FLOPS = 2 * K * H * S + 2 * 2 * H * N * M
 
 
 def tile_list_mode_pick_scores_kernel(
@@ -37,7 +38,7 @@ def tile_list_mode_pick_scores_kernel(
         psum = ctx.enter_context(tc.psum_pool(name="psum", bufs=1))
 
         def load_list(src, name):
-            tile = lists.tile([P, S // 16], U16, name=name)
+            tile = lists.tile([P, S // GROUP], U16, name=name)
             nc.sync.dma_start(tile[:], src)
             return tile
 
@@ -49,33 +50,33 @@ def tile_list_mode_pick_scores_kernel(
                 )
 
         def bank(i):
-            return psum.tile([P, HALF], F32, tag="bank%d" % (i % BANKS), name="bank%d" % (i % BANKS))
+            return psum.tile([P, BANK], F32, tag="bank%d" % (i % BANKS), name="bank%d" % (i % BANKS))
 
         idx1 = load_list(offs, "idx1")
         idx2 = load_list(offs2, "idx2")
         idx3 = load_list(offs3, "idx3")
         gain_t = keep.tile([P, 2, PACK], F32, name="gain_t")
-        nc.sync.dma_start(gain_t[:], gain.rearrange("(b p i) -> p b i", b=2, i=PACK))
+        nc.sync.dma_start(gain_t[:], gain.rearrange("(b p t) -> p b t", b=2, t=PACK))
 
-        tab_sc = keep.tile([P, T], U8, tag="stage", name="tab_sc", align_bytes=64)
+        tab_sc = keep.tile([P, T], U8, tag="w1_0_scales", name="tab_sc", align_bytes=64)
         nc.vector.memset(tab_sc[:].bitcast(I32), 0)
         nc.scalar.dma_start(tab_sc[4:P:8, :].bitcast(I32), tab_scales[0].bitcast(I32))
         load_scale_rows(nc.scalar, tab_sc, tab_scales[1:2], 1)
 
-        w2_sc_raw = keep.tile([P, H], U8, tag="small", name="w2_sc_raw", align_bytes=64)
+        w2_sc_raw = keep.tile([P, H], U8, name="w2_sc_raw", align_bytes=64)
         nc.vector.memset(w2_sc_raw[:].bitcast(I32), 0)
         load_scale_rows(nc.scalar, w2_sc_raw, w2_scales, 1)
 
-        w2_raw = keep.tile([P, 2 * H], U8, tag="big1", name="w2_raw")
+        w2_raw = keep.tile([P, 2 * H], U8, tag="stage1", name="w2_raw", align_bytes=64)
         nc.sync.dma_start(w2_raw[:].bitcast(I32), w2_words[0].bitcast(I32))
 
         def load_tab(a):
-            tile = keep.tile([P, T], I32, tag="big%d" % a, name="tab%d" % a)
+            tile = keep.tile([P, T], I32, tag="stage%d" % a, name="tab%d" % a, align_bytes=64)
             nc.sync.dma_start(tile[:], tab_words[a].rearrange("p t i -> p (t i)").bitcast(I32))
             return tile
 
         def load_weight(src, name, tag):
-            raw = keep.tile([P, PACK, HALF], F32, tag=tag, name=name, align_bytes=64)
+            raw = keep.tile([P, PACK, K_PASS], F32, tag=tag, name=name, align_bytes=64)
             nc.sync.dma_start(raw[:], src.rearrange("(p j) c -> p j c", j=PACK))
             return raw
 
@@ -86,7 +87,7 @@ def tile_list_mode_pick_scores_kernel(
             return codes, scales
 
         def round_w1(raw, name):
-            grouped = ring.tile([P, HALF * PACK], BF16, tag="w_bf", name=name, align_bytes=64)
+            grouped = keep.tile([P, K_PASS * PACK], BF16, tag=name, name=name, align_bytes=64)
             nc.scalar.copy(
                 grouped[:].rearrange("p (t m j) -> p m j t", t=PACK, j=PACK),
                 raw[:].rearrange("p j (m t) -> p m j t", t=PACK),
@@ -94,7 +95,7 @@ def tile_list_mode_pick_scores_kernel(
             return grouped
 
         def round_w3(raw, name):
-            grouped = ring.tile([P, HALF * PACK], BF16, tag="w_bf", name=name, align_bytes=64)
+            grouped = ring.tile([P, N * PACK], BF16, tag="w3_bf", name=name, align_bytes=64)
             nc.scalar.copy(
                 grouped[:].rearrange("p (c i j) -> p c j i", i=PACK, j=PACK),
                 raw[:].rearrange("p j (c i) -> p c j i", i=PACK),
@@ -102,7 +103,7 @@ def tile_list_mode_pick_scores_kernel(
             return grouped
 
         tab = [load_tab(0)]
-        w1_raw = load_weight(w1[:, 0:HALF], "w1_raw0", "first")
+        w1_raw = load_weight(w1[:, 0:K_PASS], "w1_raw0", "w1_raw0")
 
         pages = []
         for i in range(2):
@@ -116,39 +117,39 @@ def tile_list_mode_pick_scores_kernel(
             w2_raw[:].rearrange("p (b m t e) -> p b t m e", b=2, t=PACK, e=2),
         )
         tab.append(load_tab(1))
-        w2_sc = keep.tile([P, H], U8, name="w2_sc", align_bytes=64)
-        nc.vector.tensor_copy(
-            w2_sc[:].rearrange("p (b t m) -> p b t m", b=2, t=PACK),
-            w2_sc_raw[:].rearrange("p (b m t) -> p b t m", b=2, t=PACK),
-        )
 
         v_codes = {}
 
         def gather_words(a, h):
-            cols = idx1[:, h * (HALF // 16) : (h + 1) * (HALF // 16)]
-            tile = keep.tile([P, HALF], U32, name="v_codes%d%d" % (a, h), align_bytes=64)
-            nc.vector.tensor_copy(tile[:], tab[a][:].bitcast(U32).indirect(cols))
+            entries = idx1[:, h * (BANK // GROUP) : (h + 1) * (BANK // GROUP)]
+            tile = keep.tile([P, BANK], U32, name="v_codes%d%d" % (a, h), align_bytes=64)
+            nc.vector.tensor_copy(tile[:], tab[a][:].bitcast(U32).indirect(entries))
             v_codes[a, h] = tile
 
-        picked_sc = keep.tile([P, S], U8, name="picked_sc", align_bytes=64)
-        nc.vector.tensor_copy(picked_sc[:], tab_sc[:].indirect(idx1[:]))
-        v_sc = keep.tile([P, S], U8, name="v_sc", align_bytes=64)
-        nc.vector.memset(v_sc[:].bitcast(I32), 0)
+        lower_sc = keep.tile([P, S], U8, name="lower_sc", align_bytes=64)
+        nc.vector.tensor_copy(lower_sc[:], tab_sc[:].indirect(idx1[:]))
+        upper_sc = keep.tile([P, S], U8, name="upper_sc", align_bytes=64)
+        nc.vector.memset(upper_sc[:].bitcast(I32), 0)
         for r in range(4):
-            nc.scalar.dma_start(v_sc[r:P:32, :].bitcast(I32), picked_sc[4 + 8 * r : P : 32, :].bitcast(I32))
+            nc.scalar.dma_start(upper_sc[r:P:32, :].bitcast(I32), lower_sc[4 + 8 * r : P : 32, :].bitcast(I32))
 
-        w1_q = [quantize(round_w1(w1_raw, "w1_bf0"), HALF, "w1_0")]
-        wgs_t = keep.tile([P, S], F32, tag="first", name="wgs_t", align_bytes=64)
+        w1_q = [quantize(round_w1(w1_raw, "w1_bf0"), K_PASS, "w1_0")]
+        w2_sc = keep.tile([P, H], U8, tag="w1_raw0", name="w2_sc", align_bytes=64)
+        nc.vector.tensor_copy(
+            w2_sc[:].rearrange("p (b t m) -> p b t m", b=2, t=PACK),
+            w2_sc_raw[:].rearrange("p (b m t) -> p b t m", b=2, t=PACK),
+        )
+        wgs_t = keep.tile([P, S], F32, tag="w1_bf0", name="wgs_t", align_bytes=64)
         nc.sync.dma_start(wgs_t[:], wgs)
         for h in range(2):
             gather_words(0, h)
             gather_words(1, h)
 
-        w1_raw = load_weight(w1[:, HALF:H], "w1_raw1", "stage")
+        w1_raw = load_weight(w1[:, K_PASS:H], "w1_raw1", "stage1")
 
         def load_env(b):
-            tile = keep.tile([P, PACK, M], F32, tag="big%d" % b, name="env%d" % b)
-            nc.sync.dma_start(tile[:], env[b * K_PASS : (b + 1) * K_PASS, :].rearrange("(p i) m -> p i m", i=PACK))
+            tile = keep.tile([P, PACK, M], F32, tag="w1_%d_codes" % b, name="env%d" % b, align_bytes=64)
+            nc.sync.dma_start(tile[:], env[b * K_PASS : (b + 1) * K_PASS, :].rearrange("(p t) m -> p t m", t=PACK))
             return tile
 
         picked = [keep.tile([P, PACK, M], F32, name="picked%d" % b) for b in range(2)]
@@ -160,36 +161,37 @@ def tile_list_mode_pick_scores_kernel(
             codes, scales = w1_q[b]
             cols = slice(t * P, (t + 1) * P)
             act = picked[b][:, t ^ 1, :]
-            for first in range(lo, hi, HALF):
-                last = min(first + HALF, hi)
-                h, start = divmod(first, HALF)
-                part = slice(start, start + last - first)
+            for first in range(lo, hi, BANK):
+                end = min(first + BANK, hi)
+                h, start = divmod(first, BANK)
+                part = slice(start, start + end - first)
                 acc = bank(len(used_banks))
                 used_banks.append(acc)
                 nc.tensor.matmul_mx(
-                    out=acc[:, 0 : last - first], lhsT=codes[:, cols].bitcast(FP8X4), lhsT_scale=scales[:, cols],
-                    rhs=v_codes[0, h][:, part].bitcast(FP8X4), rhs_scale=v_sc[:, first:last],
+                    out=acc[:, 0 : end - first], lhsT=codes[:, cols].bitcast(FP8X4), lhsT_scale=scales[:, cols],
+                    rhs=v_codes[0, h][:, part].bitcast(FP8X4), rhs_scale=upper_sc[:, first:end],
                     start=True, stop=False,
                 )
                 nc.tensor.matmul_mx(
-                    out=acc[:, 0 : last - first], lhsT=w2_codes[:, 2 * s * P : 2 * (s + 1) * P].bitcast(FP4X4),
+                    out=acc[:, 0 : end - first], lhsT=w2_codes[:, 2 * s * P : 2 * (s + 1) * P].bitcast(FP4X4),
                     lhsT_scale=w2_sc[:, s * P : (s + 1) * P],
-                    rhs=v_codes[1, h][:, part].bitcast(FP8X4), rhs_scale=picked_sc[:, first:last],
+                    rhs=v_codes[1, h][:, part].bitcast(FP8X4), rhs_scale=lower_sc[:, first:end],
                     start=False, stop=True,
                 )
-                nc.scalar.activation(act[:, first:last], acc[:, 0 : last - first], ACT.Silu)
+                nc.scalar.activation(act[:, first:end], acc[:, 0 : end - first], ACT.Silu)
             nc.scalar.activation(feat[:, lo:hi], act[:, lo:hi], ACT.Copy, scale=gain_t[:, b, t : t + 1])
 
         def scatter(s, cuts):
             feat = ring.tile([P, S], F32, tag="feat", name="feat", bufs=3)
             for lo, hi in zip(cuts, cuts[1:]):
                 features(s, lo, hi, feat)
-                places = idx2[:, lo // 16 : hi // 16]
+                places = idx2[:, lo // GROUP : hi // GROUP]
                 nc.vector.tensor_tensor(pages[s % 2][:].indirect(places), feat[:, lo:hi], wgs_t[:, lo:hi], ALU.mult)
 
         def pick(s, lo, hi):
             b, t = divmod(s, PACK)
-            nc.vector.tensor_copy(picked[b][:, t, lo:hi], pages[s % 2][:].indirect(idx3[:, lo // 16 : hi // 16]))
+            places = idx3[:, lo // GROUP : hi // GROUP]
+            nc.vector.tensor_copy(picked[b][:, t, lo:hi], pages[s % 2][:].indirect(places))
 
         def limit(b, lo, hi, name):
             z = keep.tile([P, (hi - lo) * PACK], BF16, name=name, align_bytes=64)
@@ -201,37 +203,38 @@ def tile_list_mode_pick_scores_kernel(
             )
             return z
 
-        scatter(0, (0, CHUNK, HALF, S))
-        scatter(1, (0, S))
-        w1_q.append(quantize(round_w1(w1_raw, "w1_bf1"), HALF, "w1_1"))
-        env_t = [load_env(0)]
-        w3_raw = load_weight(w3[0:K_PASS, :], "w3_raw0", "stage")
+        whole = (0, S)
+        scatter(0, (0, CHUNK, BANK, S))
+        scatter(1, whole)
+        w1_q.append(quantize(round_w1(w1_raw, "w1_bf1"), K_PASS, "w1_1"))
+        w3_raw = load_weight(w3[0:K_PASS, :], "w3_raw0", "stage1")
         pick(0, 0, M)
         pick(1, 0, M)
-        scatter(2, (0, S))
-        scatter(3, (0, S))
-        w4_t = keep.tile([P, 2, N], I32, tag="w1_0_codes", name="w4_t", align_bytes=64)
+        scatter(2, whole)
+        scatter(3, whole)
+        env_t = [load_env(0)]
+        w4_t = keep.tile([P, 2, N], I32, tag="w1_bf1", name="w4_t", align_bytes=64)
         nc.sync.dma_start(w4_t[:], w4_words.rearrange("a p c i -> p a (c i)").bitcast(I32))
         w4_sc = keep.tile([P, 2 * N], U8, tag="w1_0_scales", name="w4_sc", align_bytes=64)
-        nc.vector.memset(w4_sc[:].bitcast(I32), 0)
+        nc.gpsimd.memset(w4_sc[:].bitcast(I32), 0)
         load_scale_rows(nc.sync, w4_sc, w4_scales, 2)
-        b3_t = keep.tile([P, N // P], F32, tag="small", name="b3_t", align_bytes=64)
-        with nc.allow_non_contiguous_dma(reason="one bias value a partition"):
-            nc.sync.dma_start(b3_t[:], b3.rearrange("(j p) -> p j", p=P))
         w3_q = [quantize(round_w3(w3_raw, "w3_bf0"), N, "w3_0")]
-        w3_raw = load_weight(w3[K_PASS:H, :], "w3_raw1", "stage")
-        env_t.append(load_env(1))
+        w3_raw = load_weight(w3[K_PASS:H, :], "w3_raw1", "stage1")
         pick(2, 0, M)
         pick(3, 0, M)
-        scatter(4, (0, S))
+        scatter(4, whole)
         z0 = limit(0, 0, M, "z0")
-        scatter(5, (0, S))
+        scatter(5, whole)
         z0_q = quantize(z0, M, "z0")
         w3_q.append(quantize(round_w3(w3_raw, "w3_bf1"), N, "w3_1"))
+        b3_t = keep.tile([P, N // P], F32, tag="stage1", name="b3_t", align_bytes=64)
+        with nc.allow_non_contiguous_dma(reason="one bias value a partition for each tile of output rows"):
+            nc.sync.dma_start(b3_t[:], b3.rearrange("(j p) -> p j", p=P))
         pick(4, 0, M)
         pick(5, 0, M)
-        scatter(6, (0, S))
-        scatter(7, (0, S))
+        scatter(6, whole)
+        scatter(7, whole)
+        env_t.append(load_env(1))
         pick(6, 0, M)
 
         def score_pass(acc, b, j, z_codes, z_scales):
@@ -246,44 +249,43 @@ def tile_list_mode_pick_scores_kernel(
                 rhs=z_codes.bitcast(FP8X4), rhs_scale=z_scales, start=False, stop=(b == 1),
             )
 
-        tiles_n = N // P
+        row_tiles = N // P
         chunks = M // CHUNK
+        open_chunks = BANKS // row_tiles
         accs = {}
 
         def open_scores(c):
-            for j in range(tiles_n):
-                accs[c, j] = bank(c * tiles_n + j)
+            for j in range(row_tiles):
+                accs[c, j] = bank(c * row_tiles + j)
                 lo = c * CHUNK
                 score_pass(accs[c, j], 0, j, z0_q[0][:, lo : lo + CHUNK], z0_q[1][:, lo : lo + CHUNK])
 
         def close_scores(c, z_q):
-            for j in range(tiles_n):
+            for j in range(row_tiles):
                 score_pass(accs[c, j], 1, j, z_q[0][:], z_q[1][:])
 
         def finish(c):
-            for j in range(tiles_n):
-                size = ring.tile([P, CHUNK], F32, tag="size", name="size", bufs=4)
+            for j in range(row_tiles):
+                size = ring.tile([P, CHUNK], F32, tag="size", name="size", bufs=row_tiles)
                 nc.scalar.activation(size[:], accs[c, j][:, CHUNK : 2 * CHUNK], ACT.Abs)
-                res = ring.tile([P, CHUNK], F32, tag="res", name="res", bufs=8)
+                res = ring.tile([P, CHUNK], F32, tag="res", name="res", bufs=2 * row_tiles)
                 nc.vector.scalar_tensor_tensor(
                     res[:], accs[c, j][:, 0:CHUNK], b3_t[:, j : j + 1], size[:], ALU.add, ALU.max
                 )
                 nc.sync.dma_start(out[j * P : (j + 1) * P, c * CHUNK : (c + 1) * CHUNK], res[:])
 
-        open_scores(0)
-        open_scores(1)
-        z1 = {}
-        pick(7, 0, CHUNK)
-        for c in range(chunks + 1):
-            if c + 1 < chunks:
-                pick(7, (c + 1) * CHUNK, (c + 2) * CHUNK)
-            if c < chunks:
-                z1[c] = limit(1, c * CHUNK, (c + 1) * CHUNK, "z1_%d" % c)
-            if c >= 1:
-                z_q = quantize(z1[c - 1], CHUNK, "z1_%d" % (c - 1))
-                if c - 1 >= 2:
-                    finish(c - 3)
-                    open_scores(c - 1)
-                close_scores(c - 1, z_q)
-        finish(chunks - 2)
-        finish(chunks - 1)
+        for c in range(open_chunks):
+            open_scores(c)
+        for c in range(open_chunks):
+            pick(SLICES - 1, c * CHUNK, (c + 1) * CHUNK)
+        for c in range(chunks):
+            z1 = limit(1, c * CHUNK, (c + 1) * CHUNK, "z1_%d" % c)
+            ahead = c + open_chunks
+            if ahead < chunks:
+                pick(SLICES - 1, ahead * CHUNK, (ahead + 1) * CHUNK)
+            if c >= open_chunks:
+                finish(c - open_chunks)
+                open_scores(c)
+            close_scores(c, quantize(z1, CHUNK, "z1_%d" % c))
+        for c in range(chunks - open_chunks, chunks):
+            finish(c)

from contextlib import ExitStack

import concourse.mybir as mybir

F32 = mybir.dt.float32
BF16 = mybir.dt.bfloat16
I32 = mybir.dt.int32
U32 = mybir.dt.uint32
U16 = mybir.dt.uint16
U8 = mybir.dt.uint8
FP8X4 = mybir.dt.float8_e4m3fn_x4
FP4X4 = mybir.dt.float4_e2m1fn_x4
ALU = mybir.AluOpType
ACT = mybir.ActivationFunctionType

P = 128
PACK = 4
K_PASS = P * PACK
GROUP = 16
K, T, S, H, T2, M, N = 1024, 4096, 1024, 1024, 2048, 1024, 512
BANK = 512
BANKS = 8
CHUNK = BANK // 2
SLICES = H // P

FLOPS = 2 * K * H * S + 2 * 2 * H * N * M


def tile_list_mode_pick_scores_kernel(
    tc, tab_words, tab_scales, offs, w1, w2_words, w2_scales, gain, wgs, offs2, offs3,
    env, w3, w4_words, w4_scales, b3, out,
):
    nc = tc.nc
    with ExitStack() as ctx:
        lists = ctx.enter_context(tc.tile_pool(name="lists", bufs=1))
        keep = ctx.enter_context(tc.tile_pool(name="keep", bufs=1))
        ring = ctx.enter_context(tc.tile_pool(name="ring", bufs=2))
        psum = ctx.enter_context(tc.psum_pool(name="psum", bufs=1))

        def load_list(src, name):
            tile = lists.tile([P, S // GROUP], U16, name=name)
            nc.sync.dma_start(tile[:], src)
            return tile

        def load_scale_rows(queue, tile, src, passes):
            for r in range(4):
                queue.dma_start(
                    tile[r:P:32, :].bitcast(I32).rearrange("q (a c) -> q a c", a=passes),
                    src[:, r:16:4, :].rearrange("a q c -> q a c").bitcast(I32),
                )

        def bank(i):
            return psum.tile([P, BANK], F32, tag="bank%d" % (i % BANKS), name="bank%d" % (i % BANKS))

        idx1 = load_list(offs, "idx1")
        idx2 = load_list(offs2, "idx2")
        idx3 = load_list(offs3, "idx3")
        gain_t = keep.tile([P, 2, PACK], F32, name="gain_t")
        nc.sync.dma_start(gain_t[:], gain.rearrange("(b p t) -> p b t", b=2, t=PACK))

        tab_sc = keep.tile([P, T], U8, tag="w1_0_scales", name="tab_sc", align_bytes=64)
        nc.vector.memset(tab_sc[:].bitcast(I32), 0)
        nc.scalar.dma_start(tab_sc[4:P:8, :].bitcast(I32), tab_scales[0].bitcast(I32))
        load_scale_rows(nc.scalar, tab_sc, tab_scales[1:2], 1)

        w2_sc_raw = keep.tile([P, H], U8, name="w2_sc_raw", align_bytes=64)
        nc.vector.memset(w2_sc_raw[:].bitcast(I32), 0)
        load_scale_rows(nc.scalar, w2_sc_raw, w2_scales, 1)

        w2_raw = keep.tile([P, 2 * H], U8, tag="stage1", name="w2_raw", align_bytes=64)
        nc.sync.dma_start(w2_raw[:].bitcast(I32), w2_words[0].bitcast(I32))

        def load_tab(a):
            tile = keep.tile([P, T], I32, tag="stage%d" % a, name="tab%d" % a, align_bytes=64)
            nc.sync.dma_start(tile[:], tab_words[a].rearrange("p t i -> p (t i)").bitcast(I32))
            return tile

        def load_weight(src, name, tag):
            raw = keep.tile([P, PACK, K_PASS], F32, tag=tag, name=name, align_bytes=64)
            nc.sync.dma_start(raw[:], src.rearrange("(p j) c -> p j c", j=PACK))
            return raw

        def quantize(src, words, name):
            codes = keep.tile([P, words], U32, tag=name + "_codes", name=name + "_codes", align_bytes=64)
            scales = keep.tile([P, words], U8, tag=name + "_scales", name=name + "_scales", align_bytes=64)
            nc.vector.quantize_mx(out=codes[:].bitcast(FP8X4), scales=scales[:], in_=src[:])
            return codes, scales

        def round_w1(raw, name):
            grouped = keep.tile([P, K_PASS * PACK], BF16, tag=name, name=name, align_bytes=64)
            nc.scalar.copy(
                grouped[:].rearrange("p (t m j) -> p m j t", t=PACK, j=PACK),
                raw[:].rearrange("p j (m t) -> p m j t", t=PACK),
            )
            return grouped

        def round_w3(raw, name):
            grouped = ring.tile([P, N * PACK], BF16, tag="w3_bf", name=name, align_bytes=64)
            nc.scalar.copy(
                grouped[:].rearrange("p (c i j) -> p c j i", i=PACK, j=PACK),
                raw[:].rearrange("p j (c i) -> p c j i", i=PACK),
            )
            return grouped

        tab = [load_tab(0)]
        w1_raw = load_weight(w1[:, 0:K_PASS], "w1_raw0", "w1_raw0")

        pages = []
        for i in range(2):
            page = keep.tile([P, T2], F32, name="page%d" % i)
            nc.vector.memset(page[:], 0.0)
            pages.append(page)

        w2_codes = keep.tile([P, 2 * H], U8, name="w2_codes", align_bytes=64)
        nc.vector.tensor_copy(
            w2_codes[:].rearrange("p (b t m e) -> p b t m e", b=2, t=PACK, e=2),
            w2_raw[:].rearrange("p (b m t e) -> p b t m e", b=2, t=PACK, e=2),
        )
        tab.append(load_tab(1))

        v_codes = {}

        def gather_words(a, h):
            entries = idx1[:, h * (BANK // GROUP) : (h + 1) * (BANK // GROUP)]
            tile = keep.tile([P, BANK], U32, name="v_codes%d%d" % (a, h), align_bytes=64)
            nc.vector.tensor_copy(tile[:], tab[a][:].bitcast(U32).indirect(entries))
            v_codes[a, h] = tile

        lower_sc = keep.tile([P, S], U8, name="lower_sc", align_bytes=64)
        nc.vector.tensor_copy(lower_sc[:], tab_sc[:].indirect(idx1[:]))
        upper_sc = keep.tile([P, S], U8, name="upper_sc", align_bytes=64)
        nc.vector.memset(upper_sc[:].bitcast(I32), 0)
        for r in range(4):
            nc.scalar.dma_start(upper_sc[r:P:32, :].bitcast(I32), lower_sc[4 + 8 * r : P : 32, :].bitcast(I32))

        w1_q = [quantize(round_w1(w1_raw, "w1_bf0"), K_PASS, "w1_0")]
        w2_sc = keep.tile([P, H], U8, tag="w1_raw0", name="w2_sc", align_bytes=64)
        nc.vector.tensor_copy(
            w2_sc[:].rearrange("p (b t m) -> p b t m", b=2, t=PACK),
            w2_sc_raw[:].rearrange("p (b m t) -> p b t m", b=2, t=PACK),
        )
        wgs_t = keep.tile([P, S], F32, tag="w1_bf0", name="wgs_t", align_bytes=64)
        nc.sync.dma_start(wgs_t[:], wgs)
        for h in range(2):
            gather_words(0, h)
            gather_words(1, h)

        w1_raw = load_weight(w1[:, K_PASS:H], "w1_raw1", "stage1")

        def load_env(b):
            tile = keep.tile([P, PACK, M], F32, tag="w1_%d_codes" % b, name="env%d" % b, align_bytes=64)
            nc.sync.dma_start(tile[:], env[b * K_PASS : (b + 1) * K_PASS, :].rearrange("(p t) m -> p t m", t=PACK))
            return tile

        picked = [keep.tile([P, PACK, M], F32, name="picked%d" % b) for b in range(2)]

        used_banks = []

        def features(s, lo, hi, feat):
            b, t = divmod(s, PACK)
            codes, scales = w1_q[b]
            cols = slice(t * P, (t + 1) * P)
            act = picked[b][:, t ^ 1, :]
            for first in range(lo, hi, BANK):
                end = min(first + BANK, hi)
                h, start = divmod(first, BANK)
                part = slice(start, start + end - first)
                acc = bank(len(used_banks))
                used_banks.append(acc)
                nc.tensor.matmul_mx(
                    out=acc[:, 0 : end - first], lhsT=codes[:, cols].bitcast(FP8X4), lhsT_scale=scales[:, cols],
                    rhs=v_codes[0, h][:, part].bitcast(FP8X4), rhs_scale=upper_sc[:, first:end],
                    start=True, stop=False,
                )
                nc.tensor.matmul_mx(
                    out=acc[:, 0 : end - first], lhsT=w2_codes[:, 2 * s * P : 2 * (s + 1) * P].bitcast(FP4X4),
                    lhsT_scale=w2_sc[:, s * P : (s + 1) * P],
                    rhs=v_codes[1, h][:, part].bitcast(FP8X4), rhs_scale=lower_sc[:, first:end],
                    start=False, stop=True,
                )
                nc.scalar.activation(act[:, first:end], acc[:, 0 : end - first], ACT.Silu)
            nc.scalar.activation(feat[:, lo:hi], act[:, lo:hi], ACT.Copy, scale=gain_t[:, b, t : t + 1])

        def scatter(s, cuts):
            feat = ring.tile([P, S], F32, tag="feat", name="feat", bufs=3)
            for lo, hi in zip(cuts, cuts[1:]):
                features(s, lo, hi, feat)
                places = idx2[:, lo // GROUP : hi // GROUP]
                nc.vector.tensor_tensor(pages[s % 2][:].indirect(places), feat[:, lo:hi], wgs_t[:, lo:hi], ALU.mult)

        def pick(s, lo, hi):
            b, t = divmod(s, PACK)
            places = idx3[:, lo // GROUP : hi // GROUP]
            nc.vector.tensor_copy(picked[b][:, t, lo:hi], pages[s % 2][:].indirect(places))

        def limit(b, lo, hi, name):
            z = keep.tile([P, (hi - lo) * PACK], BF16, name=name, align_bytes=64)
            nc.vector.tensor_tensor(
                z[:].rearrange("p (c i t) -> p c t i", i=PACK, t=PACK),
                picked[b][:, :, lo:hi].rearrange("p t (c i) -> p c t i", i=PACK),
                env_t[b][:, :, lo:hi].rearrange("p t (c i) -> p c t i", i=PACK),
                ALU.min,
            )
            return z

        whole = (0, S)
        scatter(0, (0, CHUNK, BANK, S))
        scatter(1, whole)
        w1_q.append(quantize(round_w1(w1_raw, "w1_bf1"), K_PASS, "w1_1"))
        w3_raw = load_weight(w3[0:K_PASS, :], "w3_raw0", "stage1")
        pick(0, 0, M)
        pick(1, 0, M)
        scatter(2, whole)
        scatter(3, whole)
        env_t = [load_env(0)]
        w4_t = keep.tile([P, 2, N], I32, tag="w1_bf1", name="w4_t", align_bytes=64)
        nc.sync.dma_start(w4_t[:], w4_words.rearrange("a p c i -> p a (c i)").bitcast(I32))
        w4_sc = keep.tile([P, 2 * N], U8, tag="w1_0_scales", name="w4_sc", align_bytes=64)
        nc.gpsimd.memset(w4_sc[:].bitcast(I32), 0)
        load_scale_rows(nc.sync, w4_sc, w4_scales, 2)
        w3_q = [quantize(round_w3(w3_raw, "w3_bf0"), N, "w3_0")]
        w3_raw = load_weight(w3[K_PASS:H, :], "w3_raw1", "stage1")
        pick(2, 0, M)
        pick(3, 0, M)
        scatter(4, whole)
        z0 = limit(0, 0, M, "z0")
        scatter(5, whole)
        z0_q = quantize(z0, M, "z0")
        w3_q.append(quantize(round_w3(w3_raw, "w3_bf1"), N, "w3_1"))
        b3_t = keep.tile([P, N // P], F32, tag="stage1", name="b3_t", align_bytes=64)
        with nc.allow_non_contiguous_dma(reason="one bias value a partition for each tile of output rows"):
            nc.sync.dma_start(b3_t[:], b3.rearrange("(j p) -> p j", p=P))
        pick(4, 0, M)
        pick(5, 0, M)
        scatter(6, whole)
        scatter(7, whole)
        env_t.append(load_env(1))
        pick(6, 0, M)

        def score_pass(acc, b, j, z_codes, z_scales):
            cols = slice(j * P, (j + 1) * P)
            nc.tensor.matmul_mx(
                out=acc[:, 0:CHUNK], lhsT=w3_q[b][0][:, cols].bitcast(FP8X4), lhsT_scale=w3_q[b][1][:, cols],
                rhs=z_codes.bitcast(FP8X4), rhs_scale=z_scales, start=(b == 0), stop=False,
            )
            nc.tensor.matmul_mx(
                out=acc[:, CHUNK : 2 * CHUNK], lhsT=w4_t[:, b, cols].bitcast(FP8X4),
                lhsT_scale=w4_sc[:, b * N + j * P : b * N + (j + 1) * P],
                rhs=z_codes.bitcast(FP8X4), rhs_scale=z_scales, start=False, stop=(b == 1),
            )

        row_tiles = N // P
        chunks = M // CHUNK
        open_chunks = BANKS // row_tiles
        accs = {}

        def open_scores(c):
            for j in range(row_tiles):
                accs[c, j] = bank(c * row_tiles + j)
                lo = c * CHUNK
                score_pass(accs[c, j], 0, j, z0_q[0][:, lo : lo + CHUNK], z0_q[1][:, lo : lo + CHUNK])

        def close_scores(c, z_q):
            for j in range(row_tiles):
                score_pass(accs[c, j], 1, j, z_q[0][:], z_q[1][:])

        def finish(c):
            for j in range(row_tiles):
                size = ring.tile([P, CHUNK], F32, tag="size", name="size", bufs=row_tiles)
                nc.scalar.activation(size[:], accs[c, j][:, CHUNK : 2 * CHUNK], ACT.Abs)
                res = ring.tile([P, CHUNK], F32, tag="res", name="res", bufs=2 * row_tiles)
                nc.vector.scalar_tensor_tensor(
                    res[:], accs[c, j][:, 0:CHUNK], b3_t[:, j : j + 1], size[:], ALU.add, ALU.max
                )
                nc.sync.dma_start(out[j * P : (j + 1) * P, c * CHUNK : (c + 1) * CHUNK], res[:])

        for c in range(open_chunks):
            open_scores(c)
        for c in range(open_chunks):
            pick(SLICES - 1, c * CHUNK, (c + 1) * CHUNK)
        for c in range(chunks):
            z1 = limit(1, c * CHUNK, (c + 1) * CHUNK, "z1_%d" % c)
            ahead = c + open_chunks
            if ahead < chunks:
                pick(SLICES - 1, ahead * CHUNK, (ahead + 1) * CHUNK)
            if c >= open_chunks:
                finish(c - open_chunks)
                open_scores(c)
            close_scores(c, quantize(z1, CHUNK, "z1_%d" % c))
        for c in range(chunks - open_chunks, chunks):
            finish(c)
